import numpy as np
import ml_dtypes


def mxq(x, axis, fmt="e4m3"):
    dtype, down = {"e4m3": (ml_dtypes.float8_e4m3fn, 7), "e5m2": (ml_dtypes.float8_e5m2, 14)}[fmt]
    v = np.moveaxis(np.asarray(x, np.float32).astype(ml_dtypes.bfloat16).astype(np.float64), axis, -1)
    blocks = v.reshape(v.shape[:-1] + (-1, 32))
    amax = np.abs(blocks).max(-1, keepdims=True)
    byte = np.maximum(np.where(amax > 0, np.frexp(amax)[1] - 1 + 127, 0) - down, 1)
    scale = np.exp2(byte - 127.0)
    codes = (blocks / scale).astype(np.float32).astype(dtype).astype(np.float64)
    return np.moveaxis((codes * scale).reshape(v.shape), -1, axis)


WIDE = False


def mx_kscale(k):
    if not WIDE:
        return np.ones(k)
    levels = np.array([10, -10, 5, -5, 0])
    if k % 512:
        return np.exp2(np.random.permutation(np.resize(levels, k // 32))).repeat(32)
    a = np.empty((k // 512, 16))
    for p in range(k // 512):
        a[p, :8] = np.random.permutation(np.resize(levels, 8))
        for g in range(8):
            far = levels[np.abs(levels - a[p, g]) >= 10]
            a[p, g + 8] = far[np.random.randint(len(far))]
    return np.exp2(a.ravel()).repeat(32)


def f64(x):
    return np.asarray(x).astype(np.float64)


def striped(idx):
    return np.tile(np.asarray(idx).reshape(-1, 16).T, (8, 1)).astype(np.uint16)


def unstriped(offs):
    return offs[:16].T.reshape(-1).astype(np.int64)


E2M1 = np.array([0.0, 0.5, 1.0, 1.5, 2.0, 3.0, 4.0, 6.0, -0.0, -0.5, -1.0, -1.5, -2.0, -3.0, -4.0, -6.0])


def pack_weight(w, fmt):
    k, n = w.shape
    w = f64(np.asarray(w, np.float32).astype(ml_dtypes.bfloat16)).reshape(k // 32, 32, n)
    amax = np.abs(w).max(1)
    if fmt == "e4m3":
        byte = np.frexp(amax)[1] - 1 + 127 - 7
    else:
        mant, ex = np.frexp(amax / 6.0)
        byte = np.where(mant > 0.5, ex, ex - 1) + 127
    byte = np.clip(np.where(amax > 0, byte, 1), 1, 254)
    scaled = (w * np.exp2(127.0 - byte)[:, None, :]).reshape(k, n).astype(np.float32)
    by_word = np.ascontiguousarray(scaled.reshape(k // 512, 128, 4, n).transpose(0, 1, 3, 2))
    if fmt == "e4m3":
        words = by_word.astype(ml_dtypes.float8_e4m3fn).view(np.uint8)
    else:
        c = by_word.astype(ml_dtypes.float4_e2m1fn).view(np.uint8) & 0xF
        words = (c[..., 0::2] | (c[..., 1::2] << 4)).reshape(k // 512, 128, 2 * n)
    return np.ascontiguousarray(words), np.ascontiguousarray(byte.astype(np.uint8).reshape(k // 512, 16, n))


def unpack_weight(words, scales, fmt):
    g, _, n = scales.shape
    words = np.ascontiguousarray(words).reshape(g, 128, n, -1)
    if fmt == "e4m3":
        vals = words.view(ml_dtypes.float8_e4m3fn).astype(np.float64)
    else:
        nib = np.empty((g, 128, n, 4), np.uint8)
        nib[..., 0::2] = words & 0xF
        nib[..., 1::2] = words >> 4
        vals = E2M1[nib]
    vals = vals * np.repeat(np.exp2(scales.astype(np.float64) - 127.0), 8, axis=1)[..., None]
    return vals.transpose(0, 1, 3, 2).reshape(g * 512, n)


def sigmoid(v):
    return 1.0 / (1.0 + np.exp(-v))


K, T, J, L, N = 1024, 1024, 512, 512, 512


def setup_inputs():
    n = np.random.standard_normal
    idx = np.random.permutation(T)[:J]
    fk = mx_kscale(K)
    fl = mx_kscale(L)
    xqp = pack_weight(n((K, T)) / fk[:, None], "e4m3")
    wsp = pack_weight(n((K, N)) * 1 / np.sqrt(K) * fk[:, None], "e2m1")
    xep = pack_weight(n((L, J)) / fl[:, None], "e4m3")
    return {
        "xq_words": xqp[0],
        "xq_scales": xqp[1],
        "ws_words": wsp[0],
        "ws_scales": wsp[1],
        "xe_words": xep[0],
        "xe_scales": xep[1],
        "wa": (n((L, N)) * 1 / np.sqrt(L) * fl[:, None]).astype(np.float32),
        "offs": striped(idx),
    }


def reference(xq_words, xq_scales, ws_words, ws_scales, xe_words, xe_scales, wa, offs):
    idx = unstriped(offs)
    xqu = unpack_weight(xq_words, xq_scales, "e4m3")
    wsu = unpack_weight(ws_words, ws_scales, "e2m1")
    xeu = unpack_weight(xe_words, xe_scales, "e4m3")
    u = wsu.T @ xqu
    waq = mxq(f64(wa), 0, "e4m3")
    p = waq.T @ xeu
    y = p * sigmoid(u[:, idx])
    return y

@@ -1,0 +1,156 @@
+from contextlib import ExitStack
+
+import concourse.mybir as mybir
+
+K, T, J, L, N = 1024, 1024, 512, 512, 512
+FLOPS = 2 * K * N * T + 2 * L * N * J
+
+F32 = mybir.dt.float32
+BF16 = mybir.dt.bfloat16
+I32 = mybir.dt.int32
+U32 = mybir.dt.uint32
+U16 = mybir.dt.uint16
+U8 = mybir.dt.uint8
+FP8X4 = mybir.dt.float8_e4m3fn_x4
+FP4X4 = mybir.dt.float4_e2m1fn_x4
+SIGMOID = mybir.ActivationFunctionType.Sigmoid
+MULT = mybir.AluOpType.mult
+
+P = 128
+PACK = 4
+BANK = 512
+PASSES = K // (P * PACK)
+HALVES = T // BANK
+ROW_TILES = N // P
+WA_COLS = 2 * P
+SCALAR_COPIES = ((0, 0), (0, 1), (2, 1))
+
+
+def pieces(i):
+    return [(0, J // 2), (J // 2, J)] if i == ROW_TILES - 1 else [(0, J)]
+
+
+def load_scale_rows(queue, plane, scales, r):
+    queue.dma_start(
+        out=plane[:].bitcast(I32)[r:P:32],
+        in_=scales.rearrange("z (q r) c -> r q z c", r=4)[r].bitcast(I32),
+    )
+
+
+def tile_list_expert_under_shared_gate_kernel(
+    tc, xq_words, xq_scales, ws_words, ws_scales, xe_words, xe_scales, wa, offs, out
+):
+    nc = tc.nc
+    with ExitStack() as ctx:
+        keep = ctx.enter_context(tc.tile_pool(name="keep", bufs=1))
+        psum = ctx.enter_context(tc.psum_pool(name="psum", bufs=1))
+
+        offsets = keep.tile([P, J // 16], U16, name="offsets")
+        ws_codes = keep.tile([P, PASSES, 2 * N], U8, name="ws_codes", align_bytes=64)
+        ws_plane = keep.tile([P, PASSES, N], U8, name="ws_plane", align_bytes=64)
+        xq_plane = keep.tile([P, PASSES, T], U8, name="xq_plane", align_bytes=64)
+        xe_plane = keep.tile([P, 1, J], U8, name="xe_plane", align_bytes=64)
+        xe_codes = keep.tile([P, J], U32, name="xe_codes", align_bytes=64)
+        xq_half = [keep.tile([P, PASSES, BANK], U32, name="xq_half%d" % h, align_bytes=64) for h in range(HALVES)]
+        wa_raw = [keep.tile([P, PACK, WA_COLS], F32, name="wa_raw%d" % c) for c in range(N // WA_COLS)]
+
+        for plane in (ws_plane, xq_plane, xe_plane):
+            nc.vector.memset(plane[:].bitcast(U32), 0)
+
+
+        xq_view = xq_words.rearrange("z p c r -> p z (c r)").bitcast(I32)
+        wa_view = wa.rearrange("(p j) n -> p j n", j=PACK)
+
+        nc.sync.dma_start(out=ws_codes[:].bitcast(I32), in_=ws_words.rearrange("z p c -> p z c").bitcast(I32))
+        for r in range(4):
+            load_scale_rows(nc.sync if r % 2 else nc.scalar, ws_plane, ws_scales, r)
+        for r in range(4):
+            load_scale_rows(nc.scalar, xq_plane, xq_scales, r)
+        for h in range(HALVES):
+            nc.sync.dma_start(out=xq_half[h][:].bitcast(I32), in_=xq_view[:, :, BANK * h : BANK * (h + 1)])
+        nc.sync.dma_start(out=wa_raw[0][:], in_=wa_view[:, :, 0:WA_COLS])
+        nc.sync.dma_start(out=offsets[:], in_=offs)
+        nc.sync.dma_start(out=wa_raw[1][:], in_=wa_view[:, :, WA_COLS:N])
+        nc.sync.dma_start(
+            out=xe_codes[:].bitcast(I32), in_=xe_words[0].rearrange("p c r -> p (c r)").bitcast(I32)
+        )
+        for r in range(4):
+            load_scale_rows(nc.sync, xe_plane, xe_scales, r)
+
+        def xq_codes(z, h):
+            return xq_half[h][:, z, :]
+
+        u_bank = {}
+        u_page = [keep.tile([P, T], F32, name="u_page%d" % i) for i in range(ROW_TILES)]
+        gate = [keep.tile([P, J], F32, name="gate%d" % i) for i in range(ROW_TILES)]
+        wa_codes = [keep.tile([P, WA_COLS], U32, name="wa_codes%d" % c, align_bytes=64) for c in range(2)]
+        wa_plane = [keep.tile([P, WA_COLS], U8, name="wa_plane%d" % c, align_bytes=64) for c in range(2)]
+
+        def u_pass(i, h, z):
+            if z == 0:
+                u_bank[(i, h)] = psum.tile([P, BANK], F32, name="u_bank", tag="bank%d" % (2 * i + h))
+            nc.tensor.matmul_mx(
+                out=u_bank[(i, h)][:],
+                lhsT=ws_codes[:, z, 2 * P * i : 2 * P * (i + 1)].bitcast(FP4X4),
+                lhsT_scale=ws_plane[:, z, P * i : P * (i + 1)],
+                rhs=xq_codes(z, h).bitcast(FP8X4),
+                rhs_scale=xq_plane[:, z, BANK * h : BANK * (h + 1)],
+                start=(z == 0),
+                stop=(z == PASSES - 1),
+            )
+
+        def u_copy(i, h):
+            dst = u_page[i][:, BANK * h : BANK * (h + 1)]
+            if (i, h) in SCALAR_COPIES:
+                nc.scalar.copy(out=dst, in_=u_bank[(i, h)][:])
+            else:
+                nc.vector.tensor_copy(out=dst, in_=u_bank[(i, h)][:])
+
+        def u_half(i, h):
+            for z in range(PASSES):
+                u_pass(i, h, z)
+            u_copy(i, h)
+
+        def look_up(i):
+            for lo, hi in pieces(i):
+                nc.scalar.activation(
+                    out=gate[i][:, lo:hi], in_=u_page[i][:].indirect(offsets[:, lo // 16 : hi // 16]), func=SIGMOID
+                )
+
+        def quantise_wa(c):
+            grouped = keep.tile([P, WA_COLS, PACK], BF16, name="grouped%d" % c, align_bytes=64)
+            nc.vector.tensor_copy(
+                out=grouped[:].rearrange("p (c i) t -> p c t i", i=4),
+                in_=wa_raw[c][:].rearrange("p t (c i) -> p c t i", i=4),
+            )
+            nc.vector.quantize_mx(
+                out=wa_codes[c][:].bitcast(FP8X4),
+                scales=wa_plane[c][:],
+                in_=grouped[:].rearrange("p n t -> p (n t)"),
+            )
+
+        def expert(i):
+            c, cols = i // 2, slice(P * (i % 2), P * (i % 2 + 1))
+            p_bank = psum.tile([P, J], F32, name="p_bank", tag="bank%d" % (2 * i))
+            nc.tensor.matmul_mx(
+                out=p_bank[:],
+                lhsT=wa_codes[c][:, cols].bitcast(FP8X4),
+                lhsT_scale=wa_plane[c][:, cols],
+                rhs=xe_codes[:].bitcast(FP8X4),
+                rhs_scale=xe_plane[:, 0, :],
+                start=True,
+                stop=True,
+            )
+            result = keep.tile([P, J], F32, name="result%d" % i)
+            for lo, hi in pieces(i):
+                nc.vector.tensor_tensor(out=result[:, lo:hi], in0=p_bank[:, lo:hi], in1=gate[i][:, lo:hi], op=MULT)
+                nc.sync.dma_start(out=out[P * i : P * (i + 1), lo:hi], in_=result[:, lo:hi])
+
+        quantise_wa(0)
+        for i in range(ROW_TILES):
+            for h in range(HALVES):
+                u_half(i, h)
+            look_up(i)
+        quantise_wa(1)
+        for i in range(ROW_TILES):
+            expert(i)

@@ -23,7 +23,7 @@ PASSES = K // (P * PACK)
 HALVES = T // BANK
 ROW_TILES = N // P
 WA_COLS = 2 * P
-SCALAR_COPIES = ((0, 0), (0, 1), (2, 1))
+SCALAR_COPIES = ((0, 0), (0, 1), (1, 1))
 
 
 def pieces(i):
@@ -58,6 +58,13 @@ def tile_list_expert_under_shared_gate_kernel(
             nc.vector.memset(plane[:].bitcast(U32), 0)
 
 
+        warm_in = keep.tile([P, PACK * P], BF16, name="warm_in", align_bytes=64)
+        warm_out = keep.tile([P, 1], F32, name="warm_out")
+        warm_codes = keep.tile([P, P], U32, name="warm_codes", align_bytes=64)
+        warm_plane = keep.tile([P, P], U8, name="warm_plane", align_bytes=64)
+        nc.vector.memset(warm_in[:], 1.0)
+        nc.vector.quantize_mx(out=warm_codes[:].bitcast(FP8X4), scales=warm_plane[:], in_=warm_in[:])
+
         xq_view = xq_words.rearrange("z p c r -> p z (c r)").bitcast(I32)
         wa_view = wa.rearrange("(p j) n -> p j n", j=PACK)
 
@@ -66,6 +73,7 @@ def tile_list_expert_under_shared_gate_kernel(
             load_scale_rows(nc.sync if r % 2 else nc.scalar, ws_plane, ws_scales, r)
         for r in range(4):
             load_scale_rows(nc.scalar, xq_plane, xq_scales, r)
+        nc.scalar.activation(out=warm_out[:], in_=warm_in[:, 0:1], func=SIGMOID)
         for h in range(HALVES):
             nc.sync.dma_start(out=xq_half[h][:].bitcast(I32), in_=xq_view[:, :, BANK * h : BANK * (h + 1)])
         nc.sync.dma_start(out=wa_raw[0][:], in_=wa_view[:, :, 0:WA_COLS])
@@ -145,6 +153,18 @@ def tile_list_expert_under_shared_gate_kernel(
             for lo, hi in pieces(i):
                 nc.vector.tensor_tensor(out=result[:, lo:hi], in0=p_bank[:, lo:hi], in1=gate[i][:, lo:hi], op=MULT)
                 nc.sync.dma_start(out=out[P * i : P * (i + 1), lo:hi], in_=result[:, lo:hi])
+
+        warm_bank = psum.tile([P, BANK], F32, name="warm_bank", tag="bank%d" % (2 * ROW_TILES - 1))
+        for z in range(PASSES):
+            nc.tensor.matmul_mx(
+                out=warm_bank[:],
+                lhsT=warm_codes[:].bitcast(FP8X4),
+                lhsT_scale=warm_plane[:],
+                rhs=ws_codes[:, z, :].bitcast(FP4X4),
+                rhs_scale=ws_plane[:, z, :],
+                start=(z == 0),
+                stop=(z == PASSES - 1),
+            )
 
         quantise_wa(0)
         for i in range(ROW_TILES):

from contextlib import ExitStack

import concourse.mybir as mybir

K, T, J, L, N = 1024, 1024, 512, 512, 512
FLOPS = 2 * K * N * T + 2 * L * N * J

F32 = mybir.dt.float32
BF16 = mybir.dt.bfloat16
I32 = mybir.dt.int32
U32 = mybir.dt.uint32
U16 = mybir.dt.uint16
U8 = mybir.dt.uint8
FP8X4 = mybir.dt.float8_e4m3fn_x4
FP4X4 = mybir.dt.float4_e2m1fn_x4
SIGMOID = mybir.ActivationFunctionType.Sigmoid
MULT = mybir.AluOpType.mult

P = 128
PACK = 4
BANK = 512
PASSES = K // (P * PACK)
HALVES = T // BANK
ROW_TILES = N // P
WA_COLS = 2 * P
SCALAR_COPIES = ((0, 0), (0, 1), (1, 1))


def pieces(i):
    return [(0, J // 2), (J // 2, J)] if i == ROW_TILES - 1 else [(0, J)]


def load_scale_rows(queue, plane, scales, r):
    queue.dma_start(
        out=plane[:].bitcast(I32)[r:P:32],
        in_=scales.rearrange("z (q r) c -> r q z c", r=4)[r].bitcast(I32),
    )


def tile_list_expert_under_shared_gate_kernel(
    tc, xq_words, xq_scales, ws_words, ws_scales, xe_words, xe_scales, wa, offs, out
):
    nc = tc.nc
    with ExitStack() as ctx:
        keep = ctx.enter_context(tc.tile_pool(name="keep", bufs=1))
        psum = ctx.enter_context(tc.psum_pool(name="psum", bufs=1))

        offsets = keep.tile([P, J // 16], U16, name="offsets")
        ws_codes = keep.tile([P, PASSES, 2 * N], U8, name="ws_codes", align_bytes=64)
        ws_plane = keep.tile([P, PASSES, N], U8, name="ws_plane", align_bytes=64)
        xq_plane = keep.tile([P, PASSES, T], U8, name="xq_plane", align_bytes=64)
        xe_plane = keep.tile([P, 1, J], U8, name="xe_plane", align_bytes=64)
        xe_codes = keep.tile([P, J], U32, name="xe_codes", align_bytes=64)
        xq_half = [keep.tile([P, PASSES, BANK], U32, name="xq_half%d" % h, align_bytes=64) for h in range(HALVES)]
        wa_raw = [keep.tile([P, PACK, WA_COLS], F32, name="wa_raw%d" % c) for c in range(N // WA_COLS)]

        for plane in (ws_plane, xq_plane, xe_plane):
            nc.vector.memset(plane[:].bitcast(U32), 0)


        warm_in = keep.tile([P, PACK * P], BF16, name="warm_in", align_bytes=64)
        warm_out = keep.tile([P, 1], F32, name="warm_out")
        warm_codes = keep.tile([P, P], U32, name="warm_codes", align_bytes=64)
        warm_plane = keep.tile([P, P], U8, name="warm_plane", align_bytes=64)
        nc.vector.memset(warm_in[:], 1.0)
        nc.vector.quantize_mx(out=warm_codes[:].bitcast(FP8X4), scales=warm_plane[:], in_=warm_in[:])

        xq_view = xq_words.rearrange("z p c r -> p z (c r)").bitcast(I32)
        wa_view = wa.rearrange("(p j) n -> p j n", j=PACK)

        nc.sync.dma_start(out=ws_codes[:].bitcast(I32), in_=ws_words.rearrange("z p c -> p z c").bitcast(I32))
        for r in range(4):
            load_scale_rows(nc.sync if r % 2 else nc.scalar, ws_plane, ws_scales, r)
        for r in range(4):
            load_scale_rows(nc.scalar, xq_plane, xq_scales, r)
        nc.scalar.activation(out=warm_out[:], in_=warm_in[:, 0:1], func=SIGMOID)
        for h in range(HALVES):
            nc.sync.dma_start(out=xq_half[h][:].bitcast(I32), in_=xq_view[:, :, BANK * h : BANK * (h + 1)])
        nc.sync.dma_start(out=wa_raw[0][:], in_=wa_view[:, :, 0:WA_COLS])
        nc.sync.dma_start(out=offsets[:], in_=offs)
        nc.sync.dma_start(out=wa_raw[1][:], in_=wa_view[:, :, WA_COLS:N])
        nc.sync.dma_start(
            out=xe_codes[:].bitcast(I32), in_=xe_words[0].rearrange("p c r -> p (c r)").bitcast(I32)
        )
        for r in range(4):
            load_scale_rows(nc.sync, xe_plane, xe_scales, r)

        def xq_codes(z, h):
            return xq_half[h][:, z, :]

        u_bank = {}
        u_page = [keep.tile([P, T], F32, name="u_page%d" % i) for i in range(ROW_TILES)]
        gate = [keep.tile([P, J], F32, name="gate%d" % i) for i in range(ROW_TILES)]
        wa_codes = [keep.tile([P, WA_COLS], U32, name="wa_codes%d" % c, align_bytes=64) for c in range(2)]
        wa_plane = [keep.tile([P, WA_COLS], U8, name="wa_plane%d" % c, align_bytes=64) for c in range(2)]

        def u_pass(i, h, z):
            if z == 0:
                u_bank[(i, h)] = psum.tile([P, BANK], F32, name="u_bank", tag="bank%d" % (2 * i + h))
            nc.tensor.matmul_mx(
                out=u_bank[(i, h)][:],
                lhsT=ws_codes[:, z, 2 * P * i : 2 * P * (i + 1)].bitcast(FP4X4),
                lhsT_scale=ws_plane[:, z, P * i : P * (i + 1)],
                rhs=xq_codes(z, h).bitcast(FP8X4),
                rhs_scale=xq_plane[:, z, BANK * h : BANK * (h + 1)],
                start=(z == 0),
                stop=(z == PASSES - 1),
            )

        def u_copy(i, h):
            dst = u_page[i][:, BANK * h : BANK * (h + 1)]
            if (i, h) in SCALAR_COPIES:
                nc.scalar.copy(out=dst, in_=u_bank[(i, h)][:])
            else:
                nc.vector.tensor_copy(out=dst, in_=u_bank[(i, h)][:])

        def u_half(i, h):
            for z in range(PASSES):
                u_pass(i, h, z)
            u_copy(i, h)

        def look_up(i):
            for lo, hi in pieces(i):
                nc.scalar.activation(
                    out=gate[i][:, lo:hi], in_=u_page[i][:].indirect(offsets[:, lo // 16 : hi // 16]), func=SIGMOID
                )

        def quantise_wa(c):
            grouped = keep.tile([P, WA_COLS, PACK], BF16, name="grouped%d" % c, align_bytes=64)
            nc.vector.tensor_copy(
                out=grouped[:].rearrange("p (c i) t -> p c t i", i=4),
                in_=wa_raw[c][:].rearrange("p t (c i) -> p c t i", i=4),
            )
            nc.vector.quantize_mx(
                out=wa_codes[c][:].bitcast(FP8X4),
                scales=wa_plane[c][:],
                in_=grouped[:].rearrange("p n t -> p (n t)"),
            )

        def expert(i):
            c, cols = i // 2, slice(P * (i % 2), P * (i % 2 + 1))
            p_bank = psum.tile([P, J], F32, name="p_bank", tag="bank%d" % (2 * i))
            nc.tensor.matmul_mx(
                out=p_bank[:],
                lhsT=wa_codes[c][:, cols].bitcast(FP8X4),
                lhsT_scale=wa_plane[c][:, cols],
                rhs=xe_codes[:].bitcast(FP8X4),
                rhs_scale=xe_plane[:, 0, :],
                start=True,
                stop=True,
            )
            result = keep.tile([P, J], F32, name="result%d" % i)
            for lo, hi in pieces(i):
                nc.vector.tensor_tensor(out=result[:, lo:hi], in0=p_bank[:, lo:hi], in1=gate[i][:, lo:hi], op=MULT)
                nc.sync.dma_start(out=out[P * i : P * (i + 1), lo:hi], in_=result[:, lo:hi])

        warm_bank = psum.tile([P, BANK], F32, name="warm_bank", tag="bank%d" % (2 * ROW_TILES - 1))
        for z in range(PASSES):
            nc.tensor.matmul_mx(
                out=warm_bank[:],
                lhsT=warm_codes[:].bitcast(FP8X4),
                lhsT_scale=warm_plane[:],
                rhs=ws_codes[:, z, :].bitcast(FP4X4),
                rhs_scale=ws_plane[:, z, :],
                start=(z == 0),
                stop=(z == PASSES - 1),
            )

        quantise_wa(0)
        for i in range(ROW_TILES):
            for h in range(HALVES):
                u_half(i, h)
            look_up(i)
        quantise_wa(1)
        for i in range(ROW_TILES):
            expert(i)
